import numpy as np
import ml_dtypes


def mxq(x, axis, fmt="e4m3"):
    dtype, down = {"e4m3": (ml_dtypes.float8_e4m3fn, 7), "e5m2": (ml_dtypes.float8_e5m2, 14)}[fmt]
    v = np.moveaxis(np.asarray(x, np.float32).astype(ml_dtypes.bfloat16).astype(np.float64), axis, -1)
    blocks = v.reshape(v.shape[:-1] + (-1, 32))
    amax = np.abs(blocks).max(-1, keepdims=True)
    byte = np.maximum(np.where(amax > 0, np.frexp(amax)[1] - 1 + 127, 0) - down, 1)
    scale = np.exp2(byte - 127.0)
    codes = (blocks / scale).astype(np.float32).astype(dtype).astype(np.float64)
    return np.moveaxis((codes * scale).reshape(v.shape), -1, axis)


WIDE = False


def mx_kscale(k):
    if not WIDE:
        return np.ones(k)
    levels = np.array([10, -10, 5, -5, 0])
    if k % 512:
        return np.exp2(np.random.permutation(np.resize(levels, k // 32))).repeat(32)
    a = np.empty((k // 512, 16))
    for p in range(k // 512):
        a[p, :8] = np.random.permutation(np.resize(levels, 8))
        for g in range(8):
            far = levels[np.abs(levels - a[p, g]) >= 10]
            a[p, g + 8] = far[np.random.randint(len(far))]
    return np.exp2(a.ravel()).repeat(32)


def f64(x):
    return np.asarray(x).astype(np.float64)


def striped(idx):
    return np.tile(idx.reshape(-1, 16).T, (8, 1)).astype(np.uint16)


def unstriped(offs):
    return offs[:16].T.reshape(-1).astype(np.int64)


def striped8(idx):
    return np.concatenate([x.reshape(-1, 16).T for x in idx]).astype(np.uint16)


def runs(offs, k):
    lists = np.stack([offs[16 * r : 16 * r + 16].T.reshape(-1) for r in range(8)]).astype(np.int64)
    return lists[np.arange(k) % 512 // 64]


def pack_weight(w):
    k, n = w.shape
    w = f64(np.asarray(w, np.float32).astype(ml_dtypes.bfloat16)).reshape(k // 32, 32, n)
    amax = np.abs(w).max(1)
    byte = np.clip(np.where(amax > 0, np.frexp(amax)[1] - 1 + 127 - 7, 1), 1, 254)
    scaled = (w * np.exp2(127.0 - byte)[:, None, :]).reshape(k, n).astype(np.float32)
    words = np.ascontiguousarray(scaled.reshape(k // 512, 128, 4, n).transpose(0, 1, 3, 2)).astype(ml_dtypes.float8_e4m3fn).view(np.uint8)
    return words, np.ascontiguousarray(byte.astype(np.uint8).reshape(k // 512, 16, n))


def unpack_weight(words, scales):
    g, p, n, _ = words.shape
    vals = np.ascontiguousarray(words).view(ml_dtypes.float8_e4m3fn).astype(np.float64) * np.repeat(np.exp2(scales.astype(np.float64) - 127.0), 8, axis=1)[..., None]
    return vals.transpose(0, 1, 3, 2).reshape(g * 512, n)


K, T, S, N, W = 512, 2048, 256, 512, 128


def setup_inputs():
    n = np.random.standard_normal
    s = mx_kscale(K)[:, None]
    packed_xT = pack_weight(n((K, T)) * s)
    perm = np.random.permutation(S)
    return {
        "x_words": packed_xT[0],
        "x_scales": packed_xT[1],
        "w1": (n((K, N)) / np.sqrt(2 * K) / s).astype(np.float32),
        "w2": (n((K, N)) / np.sqrt(2 * K) / s).astype(np.float32),
        "offs": striped(np.random.permutation(T)[:S]),
        "hz": striped8(np.random.randint(0, T, (8, S))),
        "n1": striped(perm[:W]),
        "n2": striped(perm[W:]),
    }


def reference(x_words, x_scales, w1, w2, offs, hz, n1, n2):
    xq = unpack_weight(x_words, x_scales)[:, unstriped(offs)]
    x_hz = unpack_weight(x_words, x_scales)[np.arange(K)[:, None], runs(hz, K)]
    h = mxq(f64(w1), 0, "e4m3").T @ xq + mxq(f64(w2), 0, "e4m3").T @ x_hz
    pb = h[:, unstriped(n2)]
    pa = h[:, unstriped(n1)]
    rb = pb - (0.5 * pa)
    ra = np.sqrt((pa) ** 2 + (pb) ** 2 + 0.25)
    ds = np.zeros((N, S))
    ds[:, unstriped(n1)] = ra
    out = ds.copy()
    out[:, unstriped(n2)] = rb
    return out

@@ -1,0 +1,147 @@
+from contextlib import ExitStack
+
+import concourse.mybir as mybir
+
+K, T, S, N, W = 512, 2048, 256, 512, 128
+FLOPS = 2 * 2 * K * N * S
+
+F32 = mybir.dt.float32
+BF16 = mybir.dt.bfloat16
+I32 = mybir.dt.int32
+U32 = mybir.dt.uint32
+U16 = mybir.dt.uint16
+U8 = mybir.dt.uint8
+FP8X4 = mybir.dt.float8_e4m3fn_x4
+ALU = mybir.AluOpType
+ACT = mybir.ActivationFunctionType
+
+P = 128
+PACK = 4
+BLK = 128
+BLOCKS = N // BLK
+
+
+def interleave(copy, grouped, raw):
+    copy(
+        out=grouped.rearrange("p (c i t) -> p c t i", i=4, t=PACK),
+        in_=raw.rearrange("p t (c i) -> p c t i", i=4),
+    )
+
+
+def tile_picked_othpolar_none_p_kernel(tc, x_words, x_scales, w1, w2, offs, hz, n1, n2, out):
+    nc = tc.nc
+    with ExitStack() as ctx:
+        keep = ctx.enter_context(tc.tile_pool(name="keep", bufs=1))
+        psum = ctx.enter_context(tc.psum_pool(name="psum", bufs=1))
+
+        lists = {}
+        for name, src in (("offs", offs), ("hz", hz), ("n1", n1), ("n2", n2)):
+            lists[name] = keep.tile(list(src.shape), U16, name="list_" + name)
+            nc.sync.dma_start(lists[name][:], src)
+
+        scale_table = keep.tile([P, T], U8, name="scale_table", tag="scale_table", align_bytes=64)
+        nc.vector.memset(scale_table[:].bitcast(I32), 0)
+        nc.scalar.dma_start(scale_table[0:P:8, :].bitcast(I32), x_scales[0].bitcast(I32))
+
+        quarter = keep.tile([P, 1], F32, name="quarter")
+        nc.vector.memset(quarter[:], 0.25)
+
+        def load_weight(name, w, c0, c1, tag):
+            raw = keep.tile([P, PACK, c1 - c0], F32, name=name, tag=tag, align_bytes=64)
+            nc.sync.dma_start(raw[:], w[:, c0:c1].rearrange("(p t) c -> p t c", t=PACK))
+            return raw
+
+        w1_first = load_weight("w1_first", w1, 0, BLK, "w1_first")
+        word_table = keep.tile([P, T], U32, name="word_table", tag="word_table", align_bytes=64)
+        nc.sync.dma_start(word_table[:].bitcast(I32), x_words[0].rearrange("p n t -> p (n t)").bitcast(I32))
+        w2_first = load_weight("w2_first", w2, 0, BLK, "w2_first")
+
+        picked_bytes = keep.tile([P, 2 * S], U8, name="picked_bytes", align_bytes=64)
+        nc.vector.tensor_copy(picked_bytes[:, S:], scale_table[:].indirect(lists["hz"][:]))
+        nc.vector.tensor_copy(picked_bytes[:, :S], scale_table[:].indirect(lists["offs"][:]))
+        x_plane = keep.tile([P, 2 * S], U8, name="x_plane", align_bytes=64)
+        nc.vector.tensor_copy(x_plane[:].bitcast(I32), picked_bytes[:].bitcast(I32))
+        for j in range(1, 4):
+            nc.scalar.dma_start(x_plane[j:P:32, :].bitcast(I32), picked_bytes[8 * j : P : 32, :].bitcast(I32))
+
+        grouped = [keep.tile([P, 2 * BLK * PACK], BF16, name="grouped%d" % b, align_bytes=64) for b in range(BLOCKS)]
+        codes = [keep.tile([P, 2 * BLK], U32, name="codes%d" % b, align_bytes=64) for b in range(BLOCKS)]
+        scales = [keep.tile([P, 2 * BLK], U8, name="scales%d" % b, align_bytes=64) for b in range(BLOCKS)]
+        acc = [psum.tile([P, S], F32, name="acc%d" % b) for b in range(BLOCKS)]
+        h = {}
+        pair = [keep.tile([P, 2 * W], F32, name="pair%d" % b) for b in range(BLOCKS)]
+        squares = [keep.tile([P, 2 * W], F32, name="squares%d" % b) for b in range(BLOCKS)]
+        sums = [keep.tile([P, W], F32, name="sums%d" % b) for b in range(BLOCKS)]
+        rb = [keep.tile([P, W], F32, name="rb%d" % b) for b in range(BLOCKS)]
+        placed = [keep.tile([P, S], F32, name="placed%d" % b) for b in range(BLOCKS)]
+        half = BLK * PACK
+
+        def quantise(b, lo, hi):
+            nc.vector.quantize_mx(
+                out=codes[b][:, lo * BLK : hi * BLK].bitcast(FP8X4),
+                scales=scales[b][:, lo * BLK : hi * BLK],
+                in_=grouped[b][:, lo * half : hi * half],
+            )
+
+        picked_words = keep.tile([P, 2 * S], U32, name="picked_words", align_bytes=64)
+
+        def multiply(b):
+            for i in range(2):
+                nc.tensor.matmul_mx(
+                    out=acc[b][:],
+                    lhsT=codes[b][:, i * BLK : (i + 1) * BLK].bitcast(FP8X4),
+                    lhsT_scale=scales[b][:, i * BLK : (i + 1) * BLK],
+                    rhs=picked_words[:, i * S : (i + 1) * S].bitcast(FP8X4),
+                    rhs_scale=x_plane[:, i * S : (i + 1) * S],
+                    start=(i == 0),
+                    stop=(i == 1),
+                )
+            h[b] = keep.tile([P, S], F32, name="h%d" % b, tag="h%d" % b)
+            if b == 0:
+                nc.scalar.copy(h[b][:], acc[b][:])
+            else:
+                nc.vector.tensor_copy(h[b][:], acc[b][:])
+
+        def fetch(b):
+            nc.scalar.activation(pair[b][:, :W], h[b][:].indirect(lists["n1"][:]), ACT.Copy)
+            nc.scalar.activation(pair[b][:, W:], h[b][:].indirect(lists["n2"][:]), ACT.Copy)
+            nc.vector.scalar_tensor_tensor(rb[b][:], pair[b][:, :W], -0.5, pair[b][:, W:], ALU.mult, ALU.add)
+            nc.vector.tensor_tensor(squares[b][:], pair[b][:], pair[b][:], ALU.mult)
+            nc.vector.tensor_tensor(sums[b][:], squares[b][:, :W], squares[b][:, W:], ALU.add)
+
+        def put_rb(b):
+            nc.scalar.activation(placed[b][:].indirect(lists["n2"][:]), rb[b][:], ACT.Copy)
+
+        def put_ra(b):
+            ra = keep.tile([P, W], F32, name="ra%d" % b, tag="h%d" % (b + 1))
+            nc.scalar.activation(ra[:], sums[b][:], ACT.Sqrt, bias=quarter[:])
+            nc.scalar.activation(placed[b][:].indirect(lists["n1"][:]), ra[:], ACT.Copy)
+            nc.sync.dma_start(out[b * BLK : (b + 1) * BLK, :], placed[b][:])
+
+        interleave(nc.scalar.copy, grouped[0][:, :half], w1_first[:])
+        quantise(0, 0, 1)
+        w2_second = load_weight("w2_second", w2, BLK, 2 * BLK, "scale_table")
+        w1_second = load_weight("w1_second", w1, BLK, 2 * BLK, "w1_first")
+        interleave(nc.scalar.copy, grouped[0][:, half:], w2_first[:])
+        nc.vector.tensor_copy(picked_words[:, :S], word_table[:].indirect(lists["offs"][:]))
+        nc.vector.tensor_copy(picked_words[:, S:], word_table[:].indirect(lists["hz"][:]))
+        quantise(0, 1, 2)
+        w1_rest = load_weight("w1_rest", w1, 2 * BLK, N, "w2_first")
+        w2_rest = load_weight("w2_rest", w2, 2 * BLK, N, "word_table")
+        interleave(nc.scalar.copy, grouped[1][:, half:], w2_second[:])
+        multiply(0)
+        interleave(nc.vector.tensor_copy, grouped[1][:, :half], w1_second[:])
+        quantise(1, 0, 2)
+        fetch(0)
+        put_rb(0)
+        for b in range(1, BLOCKS):
+            multiply(b)
+            fetch(b)
+            put_ra(b - 1)
+            put_rb(b)
+            if b + 1 < BLOCKS:
+                cols = slice((b - 1) * BLK, b * BLK)
+                interleave(nc.vector.tensor_copy, grouped[b + 1][:, :half], w1_rest[:, :, cols])
+                interleave(nc.vector.tensor_copy, grouped[b + 1][:, half:], w2_rest[:, :, cols])
+                quantise(b + 1, 0, 2)
+        put_ra(BLOCKS - 1)

@@ -41,38 +41,44 @@ def tile_picked_othpolar_none_p_kernel(tc, x_words, x_scales, w1, w2, offs, hz, 
 
         scale_table = keep.tile([P, T], U8, name="scale_table", tag="scale_table", align_bytes=64)
         nc.vector.memset(scale_table[:].bitcast(I32), 0)
-        nc.scalar.dma_start(scale_table[0:P:8, :].bitcast(I32), x_scales[0].bitcast(I32))
+        nc.sync.dma_start(scale_table[0:P:8, :].bitcast(I32), x_scales[0].bitcast(I32))
 
         quarter = keep.tile([P, 1], F32, name="quarter")
         nc.vector.memset(quarter[:], 0.25)
+        warm = keep.tile([P, 1], F32, name="warm")
+        nc.scalar.activation(warm[:], quarter[:], ACT.Sqrt)
+        x_plane = keep.tile([P, 2 * S], U8, name="x_plane", align_bytes=64)
+        nc.vector.memset(x_plane[:].bitcast(I32), 0)
 
-        def load_weight(name, w, c0, c1, tag):
-            raw = keep.tile([P, PACK, c1 - c0], F32, name=name, tag=tag, align_bytes=64)
-            nc.sync.dma_start(raw[:], w[:, c0:c1].rearrange("(p t) c -> p t c", t=PACK))
-            return raw
+        def load_weight(queue, stage, at, w, c0, c1):
+            view = stage[:, at * PACK : (at + c1 - c0) * PACK].rearrange("p (t c) -> p t c", t=PACK)
+            queue.dma_start(view, w[:, c0:c1].rearrange("(p t) c -> p t c", t=PACK))
+            return view
 
-        w1_first = load_weight("w1_first", w1, 0, BLK, "w1_first")
-        word_table = keep.tile([P, T], U32, name="word_table", tag="word_table", align_bytes=64)
+        first_stage = keep.tile([P, 2 * PACK * BLK], F32, name="first_stage")
+        w1_first = load_weight(nc.scalar, first_stage, 0, w1, 0, BLK)
+        word_table = keep.tile([P, T], U32, name="word_table", align_bytes=64)
         nc.sync.dma_start(word_table[:].bitcast(I32), x_words[0].rearrange("p n t -> p (n t)").bitcast(I32))
-        w2_first = load_weight("w2_first", w2, 0, BLK, "w2_first")
+        w2_first = load_weight(nc.sync, first_stage, BLK, w2, 0, BLK)
+        second_stage = keep.tile([P, 2 * PACK * BLK], F32, name="second_stage")
+        w1_second = load_weight(nc.sync, second_stage, 0, w1, BLK, 2 * BLK)
+        w2_second = load_weight(nc.sync, second_stage, BLK, w2, BLK, 2 * BLK)
 
         picked_bytes = keep.tile([P, 2 * S], U8, name="picked_bytes", align_bytes=64)
         nc.vector.tensor_copy(picked_bytes[:, S:], scale_table[:].indirect(lists["hz"][:]))
         nc.vector.tensor_copy(picked_bytes[:, :S], scale_table[:].indirect(lists["offs"][:]))
-        x_plane = keep.tile([P, 2 * S], U8, name="x_plane", align_bytes=64)
-        nc.vector.tensor_copy(x_plane[:].bitcast(I32), picked_bytes[:].bitcast(I32))
-        for j in range(1, 4):
-            nc.scalar.dma_start(x_plane[j:P:32, :].bitcast(I32), picked_bytes[8 * j : P : 32, :].bitcast(I32))
+        for j in range(4):
+            queue = nc.sync if j % 2 == 0 else nc.scalar
+            queue.dma_start(x_plane[j:P:32, :].bitcast(I32), picked_bytes[8 * j : P : 32, :].bitcast(I32))
 
-        grouped = [keep.tile([P, 2 * BLK * PACK], BF16, name="grouped%d" % b, align_bytes=64) for b in range(BLOCKS)]
-        codes = [keep.tile([P, 2 * BLK], U32, name="codes%d" % b, align_bytes=64) for b in range(BLOCKS)]
+        grouped = [keep.tile([P, 2 * BLK * PACK], BF16, name="grouped%d" % b, tag="grouped%d" % b, align_bytes=64) for b in range(BLOCKS)]
+        codes = [keep.tile([P, 2 * BLK], U32, name="codes%d" % b, tag="codes%d" % b if b else "scale_table", align_bytes=64) for b in range(BLOCKS)]
         scales = [keep.tile([P, 2 * BLK], U8, name="scales%d" % b, align_bytes=64) for b in range(BLOCKS)]
         acc = [psum.tile([P, S], F32, name="acc%d" % b) for b in range(BLOCKS)]
         h = {}
         pair = [keep.tile([P, 2 * W], F32, name="pair%d" % b) for b in range(BLOCKS)]
-        squares = [keep.tile([P, 2 * W], F32, name="squares%d" % b) for b in range(BLOCKS)]
-        sums = [keep.tile([P, W], F32, name="sums%d" % b) for b in range(BLOCKS)]
-        rb = [keep.tile([P, W], F32, name="rb%d" % b) for b in range(BLOCKS)]
+        sums = {}
+        rb = {}
         placed = [keep.tile([P, S], F32, name="placed%d" % b) for b in range(BLOCKS)]
         half = BLK * PACK
 
@@ -105,43 +111,69 @@ def tile_picked_othpolar_none_p_kernel(tc, x_words, x_scales, w1, w2, offs, hz, 
         def fetch(b):
             nc.scalar.activation(pair[b][:, :W], h[b][:].indirect(lists["n1"][:]), ACT.Copy)
             nc.scalar.activation(pair[b][:, W:], h[b][:].indirect(lists["n2"][:]), ACT.Copy)
-            nc.vector.scalar_tensor_tensor(rb[b][:], pair[b][:, :W], -0.5, pair[b][:, W:], ALU.mult, ALU.add)
-            nc.vector.tensor_tensor(squares[b][:], pair[b][:], pair[b][:], ALU.mult)
-            nc.vector.tensor_tensor(sums[b][:], squares[b][:, :W], squares[b][:, W:], ALU.add)
+
+        def combine(b):
+            work = keep.tile([P, 3 * W], F32, name="work%d" % b, tag="grouped%d" % (b + 1), align_bytes=64)
+            rb[b], squares = work[:, :W], work[:, W:]
+            sums[b] = keep.tile([P, W], F32, name="sums%d" % b, tag="codes%d" % (b + 1), align_bytes=64)
+            nc.vector.scalar_tensor_tensor(rb[b], pair[b][:, :W], -0.5, pair[b][:, W:], ALU.mult, ALU.add)
+            nc.vector.tensor_tensor(squares, pair[b][:], pair[b][:], ALU.mult)
+            nc.vector.tensor_tensor(sums[b][:], squares[:, :W], squares[:, W:], ALU.add)
 
         def put_rb(b):
-            nc.scalar.activation(placed[b][:].indirect(lists["n2"][:]), rb[b][:], ACT.Copy)
+            nc.scalar.activation(placed[b][:].indirect(lists["n2"][:]), rb[b], ACT.Copy)
+
+        def root(b):
+            ra[b] = keep.tile([P, W], F32, name="ra%d" % b)
+            nc.scalar.activation(ra[b][:], sums[b][:], ACT.Sqrt, bias=quarter[:])
 
         def put_ra(b):
-            ra = keep.tile([P, W], F32, name="ra%d" % b, tag="h%d" % (b + 1))
-            nc.scalar.activation(ra[:], sums[b][:], ACT.Sqrt, bias=quarter[:])
-            nc.scalar.activation(placed[b][:].indirect(lists["n1"][:]), ra[:], ACT.Copy)
+            nc.scalar.activation(placed[b][:].indirect(lists["n1"][:]), ra[b][:], ACT.Copy)
             nc.sync.dma_start(out[b * BLK : (b + 1) * BLK, :], placed[b][:])
 
-        interleave(nc.scalar.copy, grouped[0][:, :half], w1_first[:])
-        quantise(0, 0, 1)
-        w2_second = load_weight("w2_second", w2, BLK, 2 * BLK, "scale_table")
-        w1_second = load_weight("w1_second", w1, BLK, 2 * BLK, "w1_first")
-        interleave(nc.scalar.copy, grouped[0][:, half:], w2_first[:])
+        def prepare(b):
+            cols = slice((b - 2) * BLK, (b - 1) * BLK)
+            interleave(nc.vector.tensor_copy, grouped[b][:, :half], w1_rest[:, :, cols])
+            interleave(nc.vector.tensor_copy, grouped[b][:, half:], w2_rest[:, :, cols])
+            quantise(b, 0, 2)
+
+        ra = {}
+        opening = keep.tile([P, half], BF16, name="opening", tag="opening", align_bytes=64)
+        interleave(nc.scalar.copy, opening[:], w1_first)
+        nc.vector.quantize_mx(out=codes[0][:, :BLK].bitcast(FP8X4), scales=scales[0][:, :BLK], in_=opening[:])
+        interleave(nc.scalar.copy, grouped[0][:, half:], w2_first)
+        later_stage = keep.tile([P, 2 * PACK * (N - 2 * BLK)], F32, name="later_stage", tag="opening", align_bytes=64)
+        w1_rest = load_weight(nc.sync, later_stage, 0, w1, 2 * BLK, N)
+        w2_rest = load_weight(nc.sync, later_stage, 2 * BLK, w2, 2 * BLK, N)
         nc.vector.tensor_copy(picked_words[:, :S], word_table[:].indirect(lists["offs"][:]))
         nc.vector.tensor_copy(picked_words[:, S:], word_table[:].indirect(lists["hz"][:]))
         quantise(0, 1, 2)
-        w1_rest = load_weight("w1_rest", w1, 2 * BLK, N, "w2_first")
-        w2_rest = load_weight("w2_rest", w2, 2 * BLK, N, "word_table")
-        interleave(nc.scalar.copy, grouped[1][:, half:], w2_second[:])
-        multiply(0)
-        interleave(nc.vector.tensor_copy, grouped[1][:, :half], w1_second[:])
+        interleave(nc.scalar.copy, grouped[1][:, :half], w1_second)
+        interleave(nc.vector.tensor_copy, grouped[1][:, half:], w2_second)
         quantise(1, 0, 2)
+        multiply(0)
+        multiply(1)
         fetch(0)
+        fetch(1)
+        combine(0)
         put_rb(0)
-        for b in range(1, BLOCKS):
-            multiply(b)
-            fetch(b)
-            put_ra(b - 1)
-            put_rb(b)
-            if b + 1 < BLOCKS:
-                cols = slice((b - 1) * BLK, b * BLK)
-                interleave(nc.vector.tensor_copy, grouped[b + 1][:, :half], w1_rest[:, :, cols])
-                interleave(nc.vector.tensor_copy, grouped[b + 1][:, half:], w2_rest[:, :, cols])
-                quantise(b + 1, 0, 2)
-        put_ra(BLOCKS - 1)
+        root(0)
+        prepare(2)
+        multiply(2)
+        combine(1)
+        put_rb(1)
+        put_ra(0)
+        root(1)
+        fetch(2)
+        prepare(3)
+        multiply(3)
+        combine(2)
+        put_ra(1)
+        put_rb(2)
+        root(2)
+        fetch(3)
+        combine(3)
+        put_ra(2)
+        put_rb(3)
+        root(3)
+        put_ra(3)

@@ -68,8 +68,7 @@ def tile_picked_othpolar_none_p_kernel(tc, x_words, x_scales, w1, w2, offs, hz, 
         nc.vector.tensor_copy(picked_bytes[:, S:], scale_table[:].indirect(lists["hz"][:]))
         nc.vector.tensor_copy(picked_bytes[:, :S], scale_table[:].indirect(lists["offs"][:]))
         for j in range(4):
-            queue = nc.sync if j % 2 == 0 else nc.scalar
-            queue.dma_start(x_plane[j:P:32, :].bitcast(I32), picked_bytes[8 * j : P : 32, :].bitcast(I32))
+            nc.scalar.dma_start(x_plane[j:P:32, :].bitcast(I32), picked_bytes[8 * j : P : 32, :].bitcast(I32))
 
         grouped = [keep.tile([P, 2 * BLK * PACK], BF16, name="grouped%d" % b, tag="grouped%d" % b, align_bytes=64) for b in range(BLOCKS)]
         codes = [keep.tile([P, 2 * BLK], U32, name="codes%d" % b, tag="codes%d" % b if b else "scale_table", align_bytes=64) for b in range(BLOCKS)]
@@ -79,7 +78,7 @@ def tile_picked_othpolar_none_p_kernel(tc, x_words, x_scales, w1, w2, offs, hz, 
         pair = [keep.tile([P, 2 * W], F32, name="pair%d" % b) for b in range(BLOCKS)]
         sums = {}
         rb = {}
-        placed = [keep.tile([P, S], F32, name="placed%d" % b) for b in range(BLOCKS)]
+        placed = {}
         half = BLK * PACK
 
         def quantise(b, lo, hi):
@@ -112,23 +111,38 @@ def tile_picked_othpolar_none_p_kernel(tc, x_words, x_scales, w1, w2, offs, hz, 
             nc.scalar.activation(pair[b][:, :W], h[b][:].indirect(lists["n1"][:]), ACT.Copy)
             nc.scalar.activation(pair[b][:, W:], h[b][:].indirect(lists["n2"][:]), ACT.Copy)
 
-        def combine(b):
+        def combine(b, total):
             work = keep.tile([P, 3 * W], F32, name="work%d" % b, tag="grouped%d" % (b + 1), align_bytes=64)
             rb[b], squares = work[:, :W], work[:, W:]
-            sums[b] = keep.tile([P, W], F32, name="sums%d" % b, tag="codes%d" % (b + 1), align_bytes=64)
             nc.vector.scalar_tensor_tensor(rb[b], pair[b][:, :W], -0.5, pair[b][:, W:], ALU.mult, ALU.add)
             nc.vector.tensor_tensor(squares, pair[b][:], pair[b][:], ALU.mult)
-            nc.vector.tensor_tensor(sums[b][:], squares[:, :W], squares[:, W:], ALU.add)
+            nc.vector.tensor_tensor(total, squares[:, :W], squares[:, W:], ALU.add)
+            placed[b] = keep.tile([P, S], F32, name="placed%d" % b)
+
+        def combine_last(b, total):
+            squares = keep.tile([P, 2 * W], F32, name="squares_last", tag="squares_last")
+            for cols in (slice(0, W), slice(W, 2 * W)):
+                nc.vector.tensor_tensor(squares[:, cols], pair[b][:, cols], pair[b][:, cols], ALU.mult)
+            nc.vector.tensor_tensor(total, squares[:, :W], squares[:, W:], ALU.add)
+            rb_last = keep.tile([P, W], F32, name="rb_last")
+            rb[b] = rb_last[:]
+            nc.vector.scalar_tensor_tensor(rb[b], pair[b][:, :W], -0.5, pair[b][:, W:], ALU.mult, ALU.add)
+            placed[b] = keep.tile([P, S], F32, name="placed%d" % b, tag="squares_last")
 
         def put_rb(b):
             nc.scalar.activation(placed[b][:].indirect(lists["n2"][:]), rb[b], ACT.Copy)
 
-        def root(b):
-            ra[b] = keep.tile([P, W], F32, name="ra%d" % b)
-            nc.scalar.activation(ra[b][:], sums[b][:], ACT.Sqrt, bias=quarter[:])
+        def open_sums(first, count):
+            return keep.tile([P, count * W], F32, name="sums%d" % first, tag="codes%d" % (first + 1), align_bytes=64)
+
+        def root(first, count, total):
+            roots = keep.tile([P, count * W], F32, name="ra%d" % first)
+            nc.scalar.activation(roots[:], total[:], ACT.Sqrt, bias=quarter[:])
+            for i in range(count):
+                ra[first + i] = roots[:, i * W : (i + 1) * W]
 
         def put_ra(b):
-            nc.scalar.activation(placed[b][:].indirect(lists["n1"][:]), ra[b][:], ACT.Copy)
+            nc.scalar.activation(placed[b][:].indirect(lists["n1"][:]), ra[b], ACT.Copy)
             nc.sync.dma_start(out[b * BLK : (b + 1) * BLK, :], placed[b][:])
 
         def prepare(b):
@@ -155,25 +169,27 @@ def tile_picked_othpolar_none_p_kernel(tc, x_words, x_scales, w1, w2, offs, hz, 
         multiply(1)
         fetch(0)
         fetch(1)
-        combine(0)
+        sums0 = open_sums(0, 1)
+        combine(0, sums0[:])
         put_rb(0)
-        root(0)
+        root(0, 1, sums0)
         prepare(2)
         multiply(2)
-        combine(1)
+        sums1 = open_sums(1, 1)
+        combine(1, sums1[:])
         put_rb(1)
         put_ra(0)
-        root(1)
+        root(1, 1, sums1)
         fetch(2)
         prepare(3)
         multiply(3)
-        combine(2)
+        sums23 = open_sums(2, 2)
+        combine(2, sums23[:, :W])
         put_ra(1)
-        put_rb(2)
-        root(2)
         fetch(3)
-        combine(3)
-        put_ra(2)
+        put_rb(2)
+        combine_last(3, sums23[:, W:])
+        root(2, 2, sums23)
         put_rb(3)
-        root(3)
+        put_ra(2)
         put_ra(3)

@@ -68,7 +68,7 @@ def tile_picked_othpolar_none_p_kernel(tc, x_words, x_scales, w1, w2, offs, hz, 
         nc.vector.tensor_copy(picked_bytes[:, S:], scale_table[:].indirect(lists["hz"][:]))
         nc.vector.tensor_copy(picked_bytes[:, :S], scale_table[:].indirect(lists["offs"][:]))
         for j in range(4):
-            nc.scalar.dma_start(x_plane[j:P:32, :].bitcast(I32), picked_bytes[8 * j : P : 32, :].bitcast(I32))
+            nc.sync.dma_start(x_plane[j:P:32, :].bitcast(I32), picked_bytes[8 * j : P : 32, :].bitcast(I32))
 
         grouped = [keep.tile([P, 2 * BLK * PACK], BF16, name="grouped%d" % b, tag="grouped%d" % b, align_bytes=64) for b in range(BLOCKS)]
         codes = [keep.tile([P, 2 * BLK], U32, name="codes%d" % b, tag="codes%d" % b if b else "scale_table", align_bytes=64) for b in range(BLOCKS)]

from contextlib import ExitStack

import concourse.mybir as mybir

K, T, S, N, W = 512, 2048, 256, 512, 128
FLOPS = 2 * 2 * K * N * S

F32 = mybir.dt.float32
BF16 = mybir.dt.bfloat16
I32 = mybir.dt.int32
U32 = mybir.dt.uint32
U16 = mybir.dt.uint16
U8 = mybir.dt.uint8
FP8X4 = mybir.dt.float8_e4m3fn_x4
ALU = mybir.AluOpType
ACT = mybir.ActivationFunctionType

P = 128
PACK = 4
BLK = 128
BLOCKS = N // BLK


def interleave(copy, grouped, raw):
    copy(
        out=grouped.rearrange("p (c i t) -> p c t i", i=4, t=PACK),
        in_=raw.rearrange("p t (c i) -> p c t i", i=4),
    )


def tile_picked_othpolar_none_p_kernel(tc, x_words, x_scales, w1, w2, offs, hz, n1, n2, out):
    nc = tc.nc
    with ExitStack() as ctx:
        keep = ctx.enter_context(tc.tile_pool(name="keep", bufs=1))
        psum = ctx.enter_context(tc.psum_pool(name="psum", bufs=1))

        lists = {}
        for name, src in (("offs", offs), ("hz", hz), ("n1", n1), ("n2", n2)):
            lists[name] = keep.tile(list(src.shape), U16, name="list_" + name)
            nc.sync.dma_start(lists[name][:], src)

        scale_table = keep.tile([P, T], U8, name="scale_table", tag="scale_table", align_bytes=64)
        nc.vector.memset(scale_table[:].bitcast(I32), 0)
        nc.sync.dma_start(scale_table[0:P:8, :].bitcast(I32), x_scales[0].bitcast(I32))

        quarter = keep.tile([P, 1], F32, name="quarter")
        nc.vector.memset(quarter[:], 0.25)
        warm = keep.tile([P, 1], F32, name="warm")
        nc.scalar.activation(warm[:], quarter[:], ACT.Sqrt)
        x_plane = keep.tile([P, 2 * S], U8, name="x_plane", align_bytes=64)
        nc.vector.memset(x_plane[:].bitcast(I32), 0)

        def load_weight(queue, stage, at, w, c0, c1):
            view = stage[:, at * PACK : (at + c1 - c0) * PACK].rearrange("p (t c) -> p t c", t=PACK)
            queue.dma_start(view, w[:, c0:c1].rearrange("(p t) c -> p t c", t=PACK))
            return view

        first_stage = keep.tile([P, 2 * PACK * BLK], F32, name="first_stage")
        w1_first = load_weight(nc.scalar, first_stage, 0, w1, 0, BLK)
        word_table = keep.tile([P, T], U32, name="word_table", align_bytes=64)
        nc.sync.dma_start(word_table[:].bitcast(I32), x_words[0].rearrange("p n t -> p (n t)").bitcast(I32))
        w2_first = load_weight(nc.sync, first_stage, BLK, w2, 0, BLK)
        second_stage = keep.tile([P, 2 * PACK * BLK], F32, name="second_stage")
        w1_second = load_weight(nc.sync, second_stage, 0, w1, BLK, 2 * BLK)
        w2_second = load_weight(nc.sync, second_stage, BLK, w2, BLK, 2 * BLK)

        picked_bytes = keep.tile([P, 2 * S], U8, name="picked_bytes", align_bytes=64)
        nc.vector.tensor_copy(picked_bytes[:, S:], scale_table[:].indirect(lists["hz"][:]))
        nc.vector.tensor_copy(picked_bytes[:, :S], scale_table[:].indirect(lists["offs"][:]))
        for j in range(4):
            nc.sync.dma_start(x_plane[j:P:32, :].bitcast(I32), picked_bytes[8 * j : P : 32, :].bitcast(I32))

        grouped = [keep.tile([P, 2 * BLK * PACK], BF16, name="grouped%d" % b, tag="grouped%d" % b, align_bytes=64) for b in range(BLOCKS)]
        codes = [keep.tile([P, 2 * BLK], U32, name="codes%d" % b, tag="codes%d" % b if b else "scale_table", align_bytes=64) for b in range(BLOCKS)]
        scales = [keep.tile([P, 2 * BLK], U8, name="scales%d" % b, align_bytes=64) for b in range(BLOCKS)]
        acc = [psum.tile([P, S], F32, name="acc%d" % b) for b in range(BLOCKS)]
        h = {}
        pair = [keep.tile([P, 2 * W], F32, name="pair%d" % b) for b in range(BLOCKS)]
        sums = {}
        rb = {}
        placed = {}
        half = BLK * PACK

        def quantise(b, lo, hi):
            nc.vector.quantize_mx(
                out=codes[b][:, lo * BLK : hi * BLK].bitcast(FP8X4),
                scales=scales[b][:, lo * BLK : hi * BLK],
                in_=grouped[b][:, lo * half : hi * half],
            )

        picked_words = keep.tile([P, 2 * S], U32, name="picked_words", align_bytes=64)

        def multiply(b):
            for i in range(2):
                nc.tensor.matmul_mx(
                    out=acc[b][:],
                    lhsT=codes[b][:, i * BLK : (i + 1) * BLK].bitcast(FP8X4),
                    lhsT_scale=scales[b][:, i * BLK : (i + 1) * BLK],
                    rhs=picked_words[:, i * S : (i + 1) * S].bitcast(FP8X4),
                    rhs_scale=x_plane[:, i * S : (i + 1) * S],
                    start=(i == 0),
                    stop=(i == 1),
                )
            h[b] = keep.tile([P, S], F32, name="h%d" % b, tag="h%d" % b)
            if b == 0:
                nc.scalar.copy(h[b][:], acc[b][:])
            else:
                nc.vector.tensor_copy(h[b][:], acc[b][:])

        def fetch(b):
            nc.scalar.activation(pair[b][:, :W], h[b][:].indirect(lists["n1"][:]), ACT.Copy)
            nc.scalar.activation(pair[b][:, W:], h[b][:].indirect(lists["n2"][:]), ACT.Copy)

        def combine(b, total):
            work = keep.tile([P, 3 * W], F32, name="work%d" % b, tag="grouped%d" % (b + 1), align_bytes=64)
            rb[b], squares = work[:, :W], work[:, W:]
            nc.vector.scalar_tensor_tensor(rb[b], pair[b][:, :W], -0.5, pair[b][:, W:], ALU.mult, ALU.add)
            nc.vector.tensor_tensor(squares, pair[b][:], pair[b][:], ALU.mult)
            nc.vector.tensor_tensor(total, squares[:, :W], squares[:, W:], ALU.add)
            placed[b] = keep.tile([P, S], F32, name="placed%d" % b)

        def combine_last(b, total):
            squares = keep.tile([P, 2 * W], F32, name="squares_last", tag="squares_last")
            for cols in (slice(0, W), slice(W, 2 * W)):
                nc.vector.tensor_tensor(squares[:, cols], pair[b][:, cols], pair[b][:, cols], ALU.mult)
            nc.vector.tensor_tensor(total, squares[:, :W], squares[:, W:], ALU.add)
            rb_last = keep.tile([P, W], F32, name="rb_last")
            rb[b] = rb_last[:]
            nc.vector.scalar_tensor_tensor(rb[b], pair[b][:, :W], -0.5, pair[b][:, W:], ALU.mult, ALU.add)
            placed[b] = keep.tile([P, S], F32, name="placed%d" % b, tag="squares_last")

        def put_rb(b):
            nc.scalar.activation(placed[b][:].indirect(lists["n2"][:]), rb[b], ACT.Copy)

        def open_sums(first, count):
            return keep.tile([P, count * W], F32, name="sums%d" % first, tag="codes%d" % (first + 1), align_bytes=64)

        def root(first, count, total):
            roots = keep.tile([P, count * W], F32, name="ra%d" % first)
            nc.scalar.activation(roots[:], total[:], ACT.Sqrt, bias=quarter[:])
            for i in range(count):
                ra[first + i] = roots[:, i * W : (i + 1) * W]

        def put_ra(b):
            nc.scalar.activation(placed[b][:].indirect(lists["n1"][:]), ra[b], ACT.Copy)
            nc.sync.dma_start(out[b * BLK : (b + 1) * BLK, :], placed[b][:])

        def prepare(b):
            cols = slice((b - 2) * BLK, (b - 1) * BLK)
            interleave(nc.vector.tensor_copy, grouped[b][:, :half], w1_rest[:, :, cols])
            interleave(nc.vector.tensor_copy, grouped[b][:, half:], w2_rest[:, :, cols])
            quantise(b, 0, 2)

        ra = {}
        opening = keep.tile([P, half], BF16, name="opening", tag="opening", align_bytes=64)
        interleave(nc.scalar.copy, opening[:], w1_first)
        nc.vector.quantize_mx(out=codes[0][:, :BLK].bitcast(FP8X4), scales=scales[0][:, :BLK], in_=opening[:])
        interleave(nc.scalar.copy, grouped[0][:, half:], w2_first)
        later_stage = keep.tile([P, 2 * PACK * (N - 2 * BLK)], F32, name="later_stage", tag="opening", align_bytes=64)
        w1_rest = load_weight(nc.sync, later_stage, 0, w1, 2 * BLK, N)
        w2_rest = load_weight(nc.sync, later_stage, 2 * BLK, w2, 2 * BLK, N)
        nc.vector.tensor_copy(picked_words[:, :S], word_table[:].indirect(lists["offs"][:]))
        nc.vector.tensor_copy(picked_words[:, S:], word_table[:].indirect(lists["hz"][:]))
        quantise(0, 1, 2)
        interleave(nc.scalar.copy, grouped[1][:, :half], w1_second)
        interleave(nc.vector.tensor_copy, grouped[1][:, half:], w2_second)
        quantise(1, 0, 2)
        multiply(0)
        multiply(1)
        fetch(0)
        fetch(1)
        sums0 = open_sums(0, 1)
        combine(0, sums0[:])
        put_rb(0)
        root(0, 1, sums0)
        prepare(2)
        multiply(2)
        sums1 = open_sums(1, 1)
        combine(1, sums1[:])
        put_rb(1)
        put_ra(0)
        root(1, 1, sums1)
        fetch(2)
        prepare(3)
        multiply(3)
        sums23 = open_sums(2, 2)
        combine(2, sums23[:, :W])
        put_ra(1)
        fetch(3)
        put_rb(2)
        combine_last(3, sums23[:, W:])
        root(2, 2, sums23)
        put_rb(3)
        put_ra(2)
        put_ra(3)
